import numpy as np, ml_dtypes
CORES = [16,32,48,64,80]
N = 5
CB = 3
def setup_inputs(rng):
    k = (rng.standard_normal((N, 128, CB * 128), dtype=np.float32) / 8).astype(ml_dtypes.bfloat16)
    kt = np.concatenate([k[:, :, 128 * c:128 * c + 128].transpose(0, 2, 1) for c in range(CB)], axis=2)
    tri = np.triu(np.ones((128, 128), np.float32)).astype(ml_dtypes.bfloat16)
    return {"q": (rng.standard_normal((N, 128, CB * 128), dtype=np.float32) / 8).astype(ml_dtypes.bfloat16), "k": k, "kt": kt, "v": rng.standard_normal((N, 128, CB * 128), dtype=np.float32).astype(ml_dtypes.bfloat16), "m": np.broadcast_to(tri, (N, 128, 128)).copy()}
def setup_inputs_big(rng):
    d = setup_inputs(rng)
    for k in ("q", "k", "kt", "v"): d[k] = (d[k].astype(np.float32) * 1024.0).astype(d[k].dtype)
    return d
def setup_inputs_small(rng):
    d = setup_inputs(rng)
    for k in ("q", "k", "kt", "v"): d[k] = (d[k].astype(np.float32) * (1 / 1024.0)).astype(d[k].dtype)
    return d
def setup_inputs_apart(rng):
    d = setup_inputs(rng)
    f = (10.0 ** rng.permutation(np.linspace(-1.5, 1.5, N))).astype(np.float32).reshape(N, 1, 1)
    for k in ("q", "k", "kt", "v"): d[k] = (d[k].astype(np.float32) * f).astype(d[k].dtype)
    return d
def reference(q, k, kt, v, m):
    Q, K, KT, V, M = q.astype(np.float64), k.astype(np.float64), kt.astype(np.float64), v.astype(np.float64), m.astype(np.float64)
    y = np.zeros((N, 128, CB * 128)); Z = np.zeros((128, 128))
    for r in range(N):
        for c in range(CB):
            s = slice(128 * c, 128 * c + 128)
            y[r][:, s] = Z.T @ Q[r][:, s] + V[r][:, s].T @ ((K[r][:, s].T @ Q[r][:, s]) * M[r])
            Z = Z + KT[r][:, s].T @ V[r][:, s]
    return {"y": y.astype(ml_dtypes.bfloat16)}

@@ -1,0 +1,118 @@
+from concourse.bass import DstId, RemoteDMATransfer
+from concourse.mybir import AluOpType
+
+N = 5
+CB = 3
+B = 128
+
+SCRATCH = {
+    "kt_s": ("sbuf", [B, CB * B], "bfloat16"),
+    "v_s": ("sbuf", [B, CB * B], "bfloat16"),
+    "q_s": ("sbuf", [B, CB * B], "bfloat16"),
+    "k_s": ("sbuf", [B, CB * B], "bfloat16"),
+    "m_s": ("sbuf", [B, B], "bfloat16"),
+    "st_s": ("sbuf", [B, B], "bfloat16"),
+    "y_s": ("sbuf", [B, CB * B], "bfloat16"),
+    "p_st": ("psum", [B, 512], "float32"),
+}
+for _c in range(CB):
+    SCRATCH["a_s%d" % _c] = ("sbuf", [B, (CB - _c) * B], "bfloat16")
+    SCRATCH["p_a%d" % _c] = ("psum", [B, 512], "float32")
+    SCRATCH["p_y%d" % _c] = ("psum", [B, 512], "float32")
+for _s in range(N - 1):
+    SCRATCH["land%d" % _s] = ("sbuf", [B, B], "bfloat16")
+
+SEMAPHORES = (["ld_kt", "ld_v", "ld_q", "ld_k", "ld_m", "st_mm", "st_cp", "y_cp", "sent", "stored"]
+              + ["a_mm%d" % c for c in range(CB)] + ["a_cp%d" % c for c in range(CB)]
+              + ["y_mm%d" % c for c in range(CB)] + ["arr%d" % s for s in range(N - 1)])
+
+
+def rank_program(g, core, T, topo):
+    rank = T.rank_of(core)
+    if rank is None:
+        return
+    sem = T.sem
+    later = list(T.cores[rank + 1:])
+
+    def blk(t, c):
+        return t[:, B * c:B * (c + 1)]
+
+    if later:
+        g.sync.dma_start(T.kt_s[:], T.kt[:]).then_inc(sem.ld_kt, 16)
+        g.scalar.dma_start(T.v_s[:], T.v[:]).then_inc(sem.ld_v, 16)
+        g.sync.dma_start(T.q_s[:], T.q[:]).then_inc(sem.ld_q, 16)
+        g.scalar.dma_start(T.k_s[:], T.k[:]).then_inc(sem.ld_k, 16)
+        g.sync.dma_start(T.m_s[:], T.m[:]).then_inc(sem.ld_m, 16)
+    else:
+        g.sync.dma_start(T.q_s[:], T.q[:]).then_inc(sem.ld_q, 16)
+        g.scalar.dma_start(T.k_s[:], T.k[:]).then_inc(sem.ld_k, 16)
+        g.sync.dma_start(T.m_s[:], T.m[:]).then_inc(sem.ld_m, 16)
+        g.scalar.dma_start(T.v_s[:], T.v[:]).then_inc(sem.ld_v, 16)
+
+    if later:
+        g.tensor.wait_ge(sem.ld_kt, 16)
+        g.tensor.wait_ge(sem.ld_v, 16)
+        for c in range(CB):
+            g.tensor.matmul(T.p_st[:, 0:B], blk(T.kt_s, c), blk(T.v_s, c), c == 0, c == CB - 1).then_inc(sem.st_mm, 1)
+        g.vector.wait_ge(sem.st_mm, CB)
+        g.vector.tensor_copy(T.st_s[:], T.p_st[:, 0:B]).then_inc(sem.st_cp, 1)
+
+        mask = topo.mask(core, later[0])
+        for d in later:
+            assert topo.may_write(core, d)
+            mask &= topo.mask(core, d)
+        engines = bin(mask).count("1")
+        ids = []
+        for d in later:
+            rid, pid, _ = topo.addr(d)
+            ids.append(DstId(rid=rid, pnc=pid))
+        g.wait_ge(sem.st_cp, 1)
+        g.remote_dma_fused(
+            [RemoteDMATransfer(dst_ids=ids, dma_engine_mask=mask, remote_sem=sem["arr%d" % rank],
+                               srcs=[T.st_s[:]], dsts=[T["land%d" % rank][:] for _ in later])],
+            local_sem=sem.sent)
+        g.wait_ge(sem.sent, engines)
+    else:
+        g.tensor.wait_ge(sem.ld_v, 16)
+
+    g.tensor.wait_ge(sem.ld_q, 16)
+    g.tensor.wait_ge(sem.ld_k, 16)
+    for cp in range(CB):
+        w = (CB - cp) * B
+        g.tensor.matmul(T["p_a%d" % cp][:, 0:w], blk(T.k_s, cp), T.q_s[:, B * cp:CB * B], True, True).then_inc(
+            sem["a_mm%d" % cp], 1)
+    g.vector.wait_ge(sem.ld_m, 16)
+    a_parts = []
+    for cp in range(CB):
+        w = (CB - cp) * B
+        a, p = T["a_s%d" % cp], T["p_a%d" % cp]
+        g.vector.wait_ge(sem["a_mm%d" % cp], 1)
+        g.vector.tensor_tensor(a[:, 0:B], p[:, 0:B], T.m_s[:], AluOpType.mult).then_inc(sem["a_cp%d" % cp], 1)
+        if w > B:
+            g.vector.tensor_copy(a[:, B:w], p[:, B:w]).then_inc(sem["a_cp%d" % cp], 1)
+        a_parts.append(2 if w > B else 1)
+
+    senders = list(range(rank - 1, -1, -1))
+    total = [c + 1 + len(senders) for c in range(CB)]
+    done = [0] * CB
+
+    def add(c, lhsT, rhs):
+        done[c] += 1
+        g.tensor.matmul(T["p_y%d" % c][:, 0:B], lhsT, rhs, done[c] == 1, done[c] == total[c]).then_inc(
+            sem["y_mm%d" % c], 1)
+
+    for cp in range(CB):
+        g.tensor.wait_ge(sem["a_cp%d" % cp], a_parts[cp])
+        for c in range(cp, CB):
+            add(c, blk(T.v_s, cp), blk(T["a_s%d" % cp], c - cp))
+    for s in senders:
+        g.tensor.wait_ge(sem["arr%d" % s], bin(topo.mask(T.cores[s], core)).count("1"))
+        for c in range(CB):
+            add(c, T["land%d" % s][:], blk(T.q_s, c))
+
+    for c in range(CB):
+        g.vector.wait_ge(sem["y_mm%d" % c], total[c])
+        g.vector.tensor_copy(blk(T.y_s, c), T["p_y%d" % c][:, 0:B]).then_inc(sem.y_cp, 1)
+    g.sync.wait_ge(sem.y_cp, CB)
+    g.sync.dma_start(T.y[:], T.y_s[:]).then_inc(sem.stored, 16)
+    g.sync.wait_ge(sem.stored, 16)

@@ -4,6 +4,8 @@ from concourse.mybir import AluOpType
 N = 5
 CB = 3
 B = 128
+MASK_TAKERS = [0, 1]
+QW = B // (N - 1)
 
 SCRATCH = {
     "kt_s": ("sbuf", [B, CB * B], "bfloat16"),
@@ -16,13 +18,17 @@ SCRATCH = {
     "p_st": ("psum", [B, 512], "float32"),
 }
 for _c in range(CB):
-    SCRATCH["a_s%d" % _c] = ("sbuf", [B, (CB - _c) * B], "bfloat16")
-    SCRATCH["p_a%d" % _c] = ("psum", [B, 512], "float32")
+    SCRATCH["a_s%d" % _c] = ("sbuf", [B, B], "bfloat16")
     SCRATCH["p_y%d" % _c] = ("psum", [B, 512], "float32")
+for _c in range(CB - 1):
+    SCRATCH["z_s%d" % _c] = ("sbuf", [B, B], "bfloat16")
+    SCRATCH["p_z%d" % _c] = ("psum", [B, 512], "float32")
+    SCRATCH["p_a%d" % _c] = ("psum", [B, 512], "float32")
 for _s in range(N - 1):
     SCRATCH["land%d" % _s] = ("sbuf", [B, B], "bfloat16")
 
-SEMAPHORES = (["ld_kt", "ld_v", "ld_q", "ld_k", "ld_m", "st_mm", "st_cp", "y_cp", "sent", "stored"]
+SEMAPHORES = (["ld_kt", "ld_v", "ld_q", "ld_k", "ld_m", "m_arr", "st_mm", "st_cp", "z_cp", "y_cp", "sent", "stored"]
+              + ["z_mm%d" % c for c in range(CB - 1)]
               + ["a_mm%d" % c for c in range(CB)] + ["a_cp%d" % c for c in range(CB)]
               + ["y_mm%d" % c for c in range(CB)] + ["arr%d" % s for s in range(N - 1)])
 
@@ -37,60 +43,73 @@ def rank_program(g, core, T, topo):
     def blk(t, c):
         return t[:, B * c:B * (c + 1)]
 
-    if later:
-        g.sync.dma_start(T.kt_s[:], T.kt[:]).then_inc(sem.ld_kt, 16)
-        g.scalar.dma_start(T.v_s[:], T.v[:]).then_inc(sem.ld_v, 16)
-        g.sync.dma_start(T.q_s[:], T.q[:]).then_inc(sem.ld_q, 16)
-        g.scalar.dma_start(T.k_s[:], T.k[:]).then_inc(sem.ld_k, 16)
-        g.sync.dma_start(T.m_s[:], T.m[:]).then_inc(sem.ld_m, 16)
-    else:
-        g.sync.dma_start(T.q_s[:], T.q[:]).then_inc(sem.ld_q, 16)
-        g.scalar.dma_start(T.k_s[:], T.k[:]).then_inc(sem.ld_k, 16)
-        g.sync.dma_start(T.m_s[:], T.m[:]).then_inc(sem.ld_m, 16)
-        g.scalar.dma_start(T.v_s[:], T.v[:]).then_inc(sem.ld_v, 16)
+    def engines(mask):
+        return bin(mask).count("1")
 
+    def write(src, dst, ranks, remote_sem):
+        mask, ids = None, []
+        for r in ranks:
+            d = T.cores[r]
+            assert topo.may_write(core, d)
+            mask = topo.mask(core, d) if mask is None else mask & topo.mask(core, d)
+            rid, pid, _ = topo.addr(d)
+            ids.append(DstId(rid=rid, pnc=pid))
+        g.remote_dma_fused(
+            [RemoteDMATransfer(dst_ids=ids, dma_engine_mask=mask, remote_sem=remote_sem,
+                               srcs=[src], dsts=[dst for _ in ranks])],
+            local_sem=sem.sent)
+        return engines(mask)
+
+    quarter = T.m_s[:, QW * rank:QW * (rank + 1)] if later else None
+    if rank in MASK_TAKERS:
+        g.sync.dma_start(quarter, T.m[:, QW * rank:QW * (rank + 1)]).then_inc(sem.ld_m, 16)
+    elif later:
+        g.sync.dma_start(T.m_s[:], T.m[:]).then_inc(sem.ld_m, 16)
+    wkt = (CB if later else CB - 1) * B
+    g.sync.dma_start(T.kt_s[:, 0:wkt], T.kt[:, 0:wkt]).then_inc(sem.ld_kt, 16)
+    g.scalar.dma_start(T.v_s[:], T.v[:]).then_inc(sem.ld_v, 16)
+    g.sync.dma_start(T.q_s[:], T.q[:]).then_inc(sem.ld_q, 16)
+    g.scalar.dma_start(T.k_s[:], T.k[:]).then_inc(sem.ld_k, 16)
+    if not later:
+        g.sync.dma_start(T.m_s[:], T.m[:]).then_inc(sem.ld_m, 16)
+
+    left = 0
     if later:
-        g.tensor.wait_ge(sem.ld_kt, 16)
-        g.tensor.wait_ge(sem.ld_v, 16)
+        g.wait_ge(sem.ld_m, 16)
+        left += write(quarter, quarter, [r for r in MASK_TAKERS if r != rank], sem.m_arr)
+
+    g.tensor.wait_ge(sem.ld_kt, 16)
+    g.tensor.wait_ge(sem.ld_v, 16)
+    if later:
         for c in range(CB):
             g.tensor.matmul(T.p_st[:, 0:B], blk(T.kt_s, c), blk(T.v_s, c), c == 0, c == CB - 1).then_inc(sem.st_mm, 1)
         g.vector.wait_ge(sem.st_mm, CB)
         g.vector.tensor_copy(T.st_s[:], T.p_st[:, 0:B]).then_inc(sem.st_cp, 1)
-
-        mask = topo.mask(core, later[0])
-        for d in later:
-            assert topo.may_write(core, d)
-            mask &= topo.mask(core, d)
-        engines = bin(mask).count("1")
-        ids = []
-        for d in later:
-            rid, pid, _ = topo.addr(d)
-            ids.append(DstId(rid=rid, pnc=pid))
         g.wait_ge(sem.st_cp, 1)
-        g.remote_dma_fused(
-            [RemoteDMATransfer(dst_ids=ids, dma_engine_mask=mask, remote_sem=sem["arr%d" % rank],
-                               srcs=[T.st_s[:]], dsts=[T["land%d" % rank][:] for _ in later])],
-            local_sem=sem.sent)
-        g.wait_ge(sem.sent, engines)
-    else:
-        g.tensor.wait_ge(sem.ld_v, 16)
+        left += write(T.st_s[:], T["land%d" % rank][:], list(range(rank + 1, N)), sem["arr%d" % rank])
+        g.wait_ge(sem.sent, left)
+
+    for c in range(CB - 1):
+        g.tensor.matmul(T["p_z%d" % c][:, 0:B], blk(T.kt_s, c), blk(T.v_s, c), True, True).then_inc(
+            sem["z_mm%d" % c], 1)
+        g.vector.wait_ge(sem["z_mm%d" % c], 1)
+        g.vector.tensor_copy(T["z_s%d" % c][:], T["p_z%d" % c][:, 0:B]).then_inc(sem.z_cp, 1)
 
     g.tensor.wait_ge(sem.ld_q, 16)
     g.tensor.wait_ge(sem.ld_k, 16)
-    for cp in range(CB):
-        w = (CB - cp) * B
-        g.tensor.matmul(T["p_a%d" % cp][:, 0:w], blk(T.k_s, cp), T.q_s[:, B * cp:CB * B], True, True).then_inc(
-            sem["a_mm%d" % cp], 1)
     g.vector.wait_ge(sem.ld_m, 16)
-    a_parts = []
-    for cp in range(CB):
-        w = (CB - cp) * B
-        a, p = T["a_s%d" % cp], T["p_a%d" % cp]
-        g.vector.wait_ge(sem["a_mm%d" % cp], 1)
-        g.vector.tensor_tensor(a[:, 0:B], p[:, 0:B], T.m_s[:], AluOpType.mult).then_inc(sem["a_cp%d" % cp], 1)
-        if w > B:
-            g.vector.tensor_copy(a[:, B:w], p[:, B:w]).then_inc(sem["a_cp%d" % cp], 1)
-        a_parts.append(2 if w > B else 1)
+    if rank in MASK_TAKERS:
+        g.vector.wait_ge(sem.m_arr, sum(engines(topo.mask(T.cores[r], core)) for r in range(N - 1) if r != rank))
+    for c in range(CB):
+        if c < CB - 1:
+            p = T["p_a%d" % c]
+        else:
+            p = T.p_st
+            if later:
+                g.tensor.wait_ge(sem.st_cp, 1)
+        g.tensor.matmul(p[:, 0:B], blk(T.k_s, c), blk(T.q_s, c), True, True).then_inc(sem["a_mm%d" % c], 1)
+        g.vector.wait_ge(sem["a_mm%d" % c], 1)
+        g.vector.tensor_tensor(T["a_s%d" % c][:], p[:, 0:B], T.m_s[:], AluOpType.mult).then_inc(sem["a_cp%d" % c], 1)
 
     senders = list(range(rank - 1, -1, -1))
     total = [c + 1 + len(senders) for c in range(CB)]
@@ -101,12 +120,15 @@ def rank_program(g, core, T, topo):
         g.tensor.matmul(T["p_y%d" % c][:, 0:B], lhsT, rhs, done[c] == 1, done[c] == total[c]).then_inc(
             sem["y_mm%d" % c], 1)
 
-    for cp in range(CB):
-        g.tensor.wait_ge(sem["a_cp%d" % cp], a_parts[cp])
-        for c in range(cp, CB):
-            add(c, blk(T.v_s, cp), blk(T["a_s%d" % cp], c - cp))
+    g.tensor.wait_ge(sem.z_cp, CB - 1)
+    for c in range(CB):
+        for cp in range(c):
+            add(c, T["z_s%d" % cp][:], blk(T.q_s, c))
+    for c in range(CB):
+        g.tensor.wait_ge(sem["a_cp%d" % c], 1)
+        add(c, blk(T.v_s, c), T["a_s%d" % c][:])
     for s in senders:
-        g.tensor.wait_ge(sem["arr%d" % s], bin(topo.mask(T.cores[s], core)).count("1"))
+        g.tensor.wait_ge(sem["arr%d" % s], engines(topo.mask(T.cores[s], core)))
         for c in range(CB):
             add(c, T["land%d" % s][:], blk(T.q_s, c))
 

from concourse.bass import DstId, RemoteDMATransfer
from concourse.mybir import AluOpType

N = 5
CB = 3
B = 128
MASK_TAKERS = [0, 1]
QW = B // (N - 1)

SCRATCH = {
    "kt_s": ("sbuf", [B, CB * B], "bfloat16"),
    "v_s": ("sbuf", [B, CB * B], "bfloat16"),
    "q_s": ("sbuf", [B, CB * B], "bfloat16"),
    "k_s": ("sbuf", [B, CB * B], "bfloat16"),
    "m_s": ("sbuf", [B, B], "bfloat16"),
    "st_s": ("sbuf", [B, B], "bfloat16"),
    "y_s": ("sbuf", [B, CB * B], "bfloat16"),
    "p_st": ("psum", [B, 512], "float32"),
}
for _c in range(CB):
    SCRATCH["a_s%d" % _c] = ("sbuf", [B, B], "bfloat16")
    SCRATCH["p_y%d" % _c] = ("psum", [B, 512], "float32")
for _c in range(CB - 1):
    SCRATCH["z_s%d" % _c] = ("sbuf", [B, B], "bfloat16")
    SCRATCH["p_z%d" % _c] = ("psum", [B, 512], "float32")
    SCRATCH["p_a%d" % _c] = ("psum", [B, 512], "float32")
for _s in range(N - 1):
    SCRATCH["land%d" % _s] = ("sbuf", [B, B], "bfloat16")

SEMAPHORES = (["ld_kt", "ld_v", "ld_q", "ld_k", "ld_m", "m_arr", "st_mm", "st_cp", "z_cp", "y_cp", "sent", "stored"]
              + ["z_mm%d" % c for c in range(CB - 1)]
              + ["a_mm%d" % c for c in range(CB)] + ["a_cp%d" % c for c in range(CB)]
              + ["y_mm%d" % c for c in range(CB)] + ["arr%d" % s for s in range(N - 1)])


def rank_program(g, core, T, topo):
    rank = T.rank_of(core)
    if rank is None:
        return
    sem = T.sem
    later = list(T.cores[rank + 1:])

    def blk(t, c):
        return t[:, B * c:B * (c + 1)]

    def engines(mask):
        return bin(mask).count("1")

    def write(src, dst, ranks, remote_sem):
        mask, ids = None, []
        for r in ranks:
            d = T.cores[r]
            assert topo.may_write(core, d)
            mask = topo.mask(core, d) if mask is None else mask & topo.mask(core, d)
            rid, pid, _ = topo.addr(d)
            ids.append(DstId(rid=rid, pnc=pid))
        g.remote_dma_fused(
            [RemoteDMATransfer(dst_ids=ids, dma_engine_mask=mask, remote_sem=remote_sem,
                               srcs=[src], dsts=[dst for _ in ranks])],
            local_sem=sem.sent)
        return engines(mask)

    quarter = T.m_s[:, QW * rank:QW * (rank + 1)] if later else None
    if rank in MASK_TAKERS:
        g.sync.dma_start(quarter, T.m[:, QW * rank:QW * (rank + 1)]).then_inc(sem.ld_m, 16)
    elif later:
        g.sync.dma_start(T.m_s[:], T.m[:]).then_inc(sem.ld_m, 16)
    wkt = (CB if later else CB - 1) * B
    g.sync.dma_start(T.kt_s[:, 0:wkt], T.kt[:, 0:wkt]).then_inc(sem.ld_kt, 16)
    g.scalar.dma_start(T.v_s[:], T.v[:]).then_inc(sem.ld_v, 16)
    g.sync.dma_start(T.q_s[:], T.q[:]).then_inc(sem.ld_q, 16)
    g.scalar.dma_start(T.k_s[:], T.k[:]).then_inc(sem.ld_k, 16)
    if not later:
        g.sync.dma_start(T.m_s[:], T.m[:]).then_inc(sem.ld_m, 16)

    left = 0
    if later:
        g.wait_ge(sem.ld_m, 16)
        left += write(quarter, quarter, [r for r in MASK_TAKERS if r != rank], sem.m_arr)

    g.tensor.wait_ge(sem.ld_kt, 16)
    g.tensor.wait_ge(sem.ld_v, 16)
    if later:
        for c in range(CB):
            g.tensor.matmul(T.p_st[:, 0:B], blk(T.kt_s, c), blk(T.v_s, c), c == 0, c == CB - 1).then_inc(sem.st_mm, 1)
        g.vector.wait_ge(sem.st_mm, CB)
        g.vector.tensor_copy(T.st_s[:], T.p_st[:, 0:B]).then_inc(sem.st_cp, 1)
        g.wait_ge(sem.st_cp, 1)
        left += write(T.st_s[:], T["land%d" % rank][:], list(range(rank + 1, N)), sem["arr%d" % rank])
        g.wait_ge(sem.sent, left)

    for c in range(CB - 1):
        g.tensor.matmul(T["p_z%d" % c][:, 0:B], blk(T.kt_s, c), blk(T.v_s, c), True, True).then_inc(
            sem["z_mm%d" % c], 1)
        g.vector.wait_ge(sem["z_mm%d" % c], 1)
        g.vector.tensor_copy(T["z_s%d" % c][:], T["p_z%d" % c][:, 0:B]).then_inc(sem.z_cp, 1)

    g.tensor.wait_ge(sem.ld_q, 16)
    g.tensor.wait_ge(sem.ld_k, 16)
    g.vector.wait_ge(sem.ld_m, 16)
    if rank in MASK_TAKERS:
        g.vector.wait_ge(sem.m_arr, sum(engines(topo.mask(T.cores[r], core)) for r in range(N - 1) if r != rank))
    for c in range(CB):
        if c < CB - 1:
            p = T["p_a%d" % c]
        else:
            p = T.p_st
            if later:
                g.tensor.wait_ge(sem.st_cp, 1)
        g.tensor.matmul(p[:, 0:B], blk(T.k_s, c), blk(T.q_s, c), True, True).then_inc(sem["a_mm%d" % c], 1)
        g.vector.wait_ge(sem["a_mm%d" % c], 1)
        g.vector.tensor_tensor(T["a_s%d" % c][:], p[:, 0:B], T.m_s[:], AluOpType.mult).then_inc(sem["a_cp%d" % c], 1)

    senders = list(range(rank - 1, -1, -1))
    total = [c + 1 + len(senders) for c in range(CB)]
    done = [0] * CB

    def add(c, lhsT, rhs):
        done[c] += 1
        g.tensor.matmul(T["p_y%d" % c][:, 0:B], lhsT, rhs, done[c] == 1, done[c] == total[c]).then_inc(
            sem["y_mm%d" % c], 1)

    g.tensor.wait_ge(sem.z_cp, CB - 1)
    for c in range(CB):
        for cp in range(c):
            add(c, T["z_s%d" % cp][:], blk(T.q_s, c))
    for c in range(CB):
        g.tensor.wait_ge(sem["a_cp%d" % c], 1)
        add(c, blk(T.v_s, c), T["a_s%d" % c][:])
    for s in senders:
        g.tensor.wait_ge(sem["arr%d" % s], engines(topo.mask(T.cores[s], core)))
        for c in range(CB):
            add(c, T["land%d" % s][:], blk(T.q_s, c))

    for c in range(CB):
        g.vector.wait_ge(sem["y_mm%d" % c], total[c])
        g.vector.tensor_copy(blk(T.y_s, c), T["p_y%d" % c][:, 0:B]).then_inc(sem.y_cp, 1)
    g.sync.wait_ge(sem.y_cp, CB)
    g.sync.dma_start(T.y[:], T.y_s[:]).then_inc(sem.stored, 16)
    g.sync.wait_ge(sem.stored, 16)
